import numpy as np
import ml_dtypes


def mxq(x, axis, fmt="e4m3"):
    dtype, down = {"e4m3": (ml_dtypes.float8_e4m3fn, 7), "e5m2": (ml_dtypes.float8_e5m2, 14)}[fmt]
    v = np.moveaxis(np.asarray(x, np.float32).astype(ml_dtypes.bfloat16).astype(np.float64), axis, -1)
    blocks = v.reshape(v.shape[:-1] + (-1, 32))
    amax = np.abs(blocks).max(-1, keepdims=True)
    byte = np.maximum(np.where(amax > 0, np.frexp(amax)[1] - 1 + 127, 0) - down, 1)
    scale = np.exp2(byte - 127.0)
    codes = (blocks / scale).astype(np.float32).astype(dtype).astype(np.float64)
    return np.moveaxis((codes * scale).reshape(v.shape), -1, axis)


WIDE = False


def mx_kscale(k):
    if not WIDE:
        return np.ones(k)
    levels = np.array([30, -30])
    if k % 512:
        return np.exp2(np.random.permutation(np.resize(levels, k // 32))).repeat(32)
    a = np.empty((k // 512, 16))
    for p in range(k // 512):
        a[p, :8] = np.random.permutation(np.resize(levels, 8))
        for g in range(8):
            far = levels[np.abs(levels - a[p, g]) >= 10]
            a[p, g + 8] = far[np.random.randint(len(far))]
    return np.exp2(a.ravel()).repeat(32)


def f64(x):
    return np.asarray(x).astype(np.float64)


def striped(idx):
    return np.tile(np.asarray(idx).reshape(-1, 16).T, (8, 1)).astype(np.uint16)


def unstriped(offs):
    return offs[:16].T.reshape(-1).astype(np.int64)


E2M1 = np.array([0.0, 0.5, 1.0, 1.5, 2.0, 3.0, 4.0, 6.0, -0.0, -0.5, -1.0, -1.5, -2.0, -3.0, -4.0, -6.0])


def pack_weight(w, fmt):
    k, n = w.shape
    w = f64(np.asarray(w, np.float32).astype(ml_dtypes.bfloat16)).reshape(k // 32, 32, n)
    amax = np.abs(w).max(1)
    if fmt in ("e4m3", "e5m2"):
        byte = np.frexp(amax)[1] - 1 + 127 - (7 if fmt == "e4m3" else 14)
    else:
        mant, ex = np.frexp(amax / 6.0)
        byte = np.where(mant > 0.5, ex, ex - 1) + 127
    byte = np.clip(np.where(amax > 0, byte, 1), 1, 254)
    scaled = (w * np.exp2(127.0 - byte)[:, None, :]).reshape(k, n).astype(np.float32)
    by_word = np.ascontiguousarray(scaled.reshape(k // 512, 128, 4, n).transpose(0, 1, 3, 2))
    if fmt in ("e4m3", "e5m2"):
        words = by_word.astype(ml_dtypes.float8_e4m3fn if fmt == "e4m3" else ml_dtypes.float8_e5m2).view(np.uint8)
    else:
        c = by_word.astype(ml_dtypes.float4_e2m1fn).view(np.uint8) & 0xF
        words = (c[..., 0::2] | (c[..., 1::2] << 4)).reshape(k // 512, 128, 2 * n)
    return np.ascontiguousarray(words), np.ascontiguousarray(byte.astype(np.uint8).reshape(k // 512, 16, n))


def unpack_weight(words, scales, fmt):
    g, _, n = scales.shape
    words = np.ascontiguousarray(words).reshape(g, 128, n, -1)
    if fmt in ("e4m3", "e5m2"):
        vals = words.view(ml_dtypes.float8_e4m3fn if fmt == "e4m3" else ml_dtypes.float8_e5m2).astype(np.float64)
    else:
        nib = np.empty((g, 128, n, 4), np.uint8)
        nib[..., 0::2] = words & 0xF
        nib[..., 1::2] = words >> 4
        vals = E2M1[nib]
    vals = vals * np.repeat(np.exp2(scales.astype(np.float64) - 127.0), 8, axis=1)[..., None]
    return vals.transpose(0, 1, 3, 2).reshape(g * 512, n)


K, T, Z, J, R, N, E = 512, 1024, 1024, 256, 512, 256, 128


def setup_inputs():
    n = np.random.standard_normal
    idx = np.random.permutation(T)[:J]
    idx2 = np.random.permutation(Z)[:J]
    idx3 = np.random.permutation(J)[:E]
    idx4 = np.random.permutation(J)[:E]
    fk = mx_kscale(K)
    fr = mx_kscale(R)
    xtp = pack_weight(n((K, T)) / fk[:, None], "e2m1")
    xop = pack_weight(n((K, Z)) / fk[:, None], "e4m3")
    wp = pack_weight(n((K, R)) * 1 / np.sqrt(K) * fk[:, None] * fr, "e4m3")
    w2p = pack_weight(n((K, R)) * 1 / np.sqrt(K) * fk[:, None] * fr, "e5m2")
    wbp = pack_weight(n((R, N)) * 1 / np.sqrt(R) / fr[:, None], "e2m1")
    return {
        "xt_words": xtp[0],
        "xt_scales": xtp[1],
        "xo_words": xop[0],
        "xo_scales": xop[1],
        "w_words": wp[0],
        "w_scales": wp[1],
        "w2_words": w2p[0],
        "w2_scales": w2p[1],
        "wb_words": wbp[0],
        "wb_scales": wbp[1],
        "offs": striped(idx),
        "offs2": striped(idx2),
        "offs3": striped(idx3),
        "offs4": striped(idx4),
    }


def reference(xt_words, xt_scales, xo_words, xo_scales, w_words, w_scales, w2_words, w2_scales, wb_words, wb_scales, offs, offs2, offs3, offs4):
    idx = unstriped(offs)
    idx2 = unstriped(offs2)
    idx3 = unstriped(offs3)
    idx4 = unstriped(offs4)
    xtu = unpack_weight(xt_words, xt_scales, "e2m1")
    xou = unpack_weight(xo_words, xo_scales, "e4m3")
    wu = unpack_weight(w_words, w_scales, "e4m3")
    w2u = unpack_weight(w2_words, w2_scales, "e5m2")
    wbu = unpack_weight(wb_words, wb_scales, "e2m1")
    xtidxg = xtu[:, idx]
    xoidx2g = xou[:, idx2]
    a = wu.T @ xtidxg + w2u.T @ xoidx2g
    b = w2u.T @ xtidxg + wu.T @ xoidx2g
    hid = np.abs(a - b)
    hidq = mxq(hid, 0, "e5m2")
    p = wbu.T @ hidq
    y = np.maximum(p[:, idx3], p[:, idx4])
    return y

@@ -1,0 +1,167 @@
+from contextlib import ExitStack
+
+import concourse.mybir as mybir
+from concourse.masks import make_identity
+
+K, T, Z, J, R, N, E = 512, 1024, 1024, 256, 512, 256, 128
+FLOPS = 4 * 2 * K * R * J + 2 * R * N * J
+
+F32 = mybir.dt.float32
+BF16 = mybir.dt.bfloat16
+I32 = mybir.dt.int32
+U32 = mybir.dt.uint32
+U16 = mybir.dt.uint16
+U8 = mybir.dt.uint8
+E4M3 = mybir.dt.float8_e4m3fn_x4
+E5M2 = mybir.dt.float8_e5m2_x4
+E2M1 = mybir.dt.float4_e2m1fn_x4
+ACT = mybir.ActivationFunctionType
+ALU = mybir.AluOpType
+
+P = 128
+PACK = 4
+QUADRANT = 32
+LIST_ROWS = 16
+JT = J // P
+NT = N // P
+
+
+def tile_list_crossed_direct_one_bestoftwo_kernel(
+    tc, xt_words, xt_scales, xo_words, xo_scales, w_words, w_scales, w2_words, w2_scales,
+    wb_words, wb_scales, offs, offs2, offs3, offs4, out
+):
+    nc = tc.nc
+    with ExitStack() as ctx:
+        lists = ctx.enter_context(tc.tile_pool(name="lists", bufs=1))
+        sb = ctx.enter_context(tc.tile_pool(name="sb", bufs=1))
+        psum = ctx.enter_context(tc.psum_pool(name="psum", bufs=1))
+
+        def load_list(src, name):
+            tile = lists.tile(list(src.shape), U16, name=name)
+            nc.sync.dma_start(tile[:], src)
+            return tile
+
+        def zeroed_plane(width, name):
+            plane = sb.tile([P, width], U8, name=name, align_bytes=64)
+            nc.vector.memset(plane[:].bitcast(I32), 0)
+            return plane
+
+        def load_scales(plane, src, queues):
+            for q, queue in enumerate(queues):
+                queue.dma_start(
+                    plane[QUADRANT * q : QUADRANT * q + PACK, :].bitcast(I32),
+                    src[0, PACK * q : PACK * (q + 1), :].bitcast(I32),
+                )
+
+        def load_fp8_words(src, name):
+            tile = sb.tile([P, src.shape[2]], U32, name=name, align_bytes=64)
+            nc.sync.dma_start(tile[:].bitcast(I32), src[0].rearrange("p n t -> p (n t)").bitcast(I32))
+            return tile
+
+        def load_fp4_words(src, name):
+            tile = sb.tile([P, src.shape[2] // 2], U16, name=name, align_bytes=64)
+            nc.sync.dma_start(tile[:].bitcast(I32), src[0].bitcast(I32))
+            return tile
+
+        xo_s = zeroed_plane(Z, "xo_s")
+        xt_s = zeroed_plane(T, "xt_s")
+        both_s = sb.tile([P, 2 * R], U8, name="both_s", align_bytes=64)
+        w2_s = both_s[:, 0:R]
+        w_s = both_s[:, R : 2 * R]
+        wb_s = sb.tile([P, N], U8, name="wb_s", align_bytes=64)
+
+        rows = K // 32
+        nc.sync.dma_start(both_s[0:rows, 0:R].bitcast(I32), w2_scales[0].bitcast(I32))
+        nc.sync.dma_start(both_s[0:rows, R : 2 * R].bitcast(I32), w_scales[0].bitcast(I32))
+        idx2 = load_list(offs2, "idx2")
+        load_scales(xo_s, xo_scales, [nc.sync] * 4)
+        xo_w = load_fp8_words(xo_words, "xo_w")
+        w_w = load_fp8_words(w_words, "w_w")
+        for q in range(1, P // QUADRANT):
+            nc.sync.dma_start(
+                both_s[QUADRANT * q : QUADRANT * q + PACK, :].bitcast(I32),
+                both_s[PACK * q : PACK * (q + 1), :].bitcast(I32),
+            )
+        w2_w = load_fp8_words(w2_words, "w2_w")
+        idx = load_list(offs, "idx")
+        xt_w = load_fp4_words(xt_words, "xt_w")
+        load_scales(xt_s, xt_scales, [nc.gpsimd] * 3 + [nc.sync])
+        load_scales(wb_s, wb_scales, [nc.sync] * 4)
+        wb_w = load_fp4_words(wb_words, "wb_w")
+        idx3 = load_list(offs3, "idx3")
+        idx4 = load_list(offs4, "idx4")
+
+        ident = sb.tile([P, P], F32, name="ident", align_bytes=64)
+        make_identity(nc, ident[:])
+
+        def gather_columns(words, plane, index, jt, name):
+            cols = P // LIST_ROWS
+            part = index[:, jt * cols : (jt + 1) * cols]
+            g_s = sb.tile([P, P], U8, name=name + "_gs%d" % jt, align_bytes=64)
+            g_w = sb.tile([P, P], words.dtype, name=name + "_gw%d" % jt, align_bytes=64)
+            nc.vector.tensor_copy(g_s[:], plane[:].indirect(part))
+            nc.vector.tensor_copy(g_w[:], words[:].indirect(part))
+            return g_w, g_s
+
+        xo_g = [gather_columns(xo_w, xo_s, idx2, jt, "xo") for jt in range(JT)]
+        xt_g = [gather_columns(xt_w, xt_s, idx, jt, "xt") for jt in range(JT)]
+
+        a_ps = [psum.tile([P, R], F32, name="a%d" % jt) for jt in range(JT)]
+        b_ps = [psum.tile([P, R], F32, name="b%d" % jt) for jt in range(JT)]
+
+        def first_stage(acc, picked, picked_fmt, words, fmt, plane, first):
+            nc.tensor.matmul_mx(
+                out=acc[:], lhsT=picked[0][:].bitcast(picked_fmt), lhsT_scale=picked[1][:],
+                rhs=words[:].bitcast(fmt), rhs_scale=plane, start=first, stop=not first,
+            )
+
+        for jt in range(JT):
+            first_stage(b_ps[jt], xo_g[jt], E4M3, w_w, E4M3, w_s, True)
+            first_stage(a_ps[jt], xo_g[jt], E4M3, w2_w, E5M2, w2_s, True)
+            first_stage(b_ps[jt], xt_g[jt], E2M1, w2_w, E5M2, w2_s, False)
+            first_stage(a_ps[jt], xt_g[jt], E2M1, w_w, E4M3, w_s, False)
+
+        half = PACK // 2
+        turned = []
+        for jt in range(JT):
+            bank = psum.tile([P, PACK, P], F32, name="turned%d" % jt)
+            for h in range(2):
+                ts = slice(h * half, (h + 1) * half)
+                b_sb = sb.tile([P, half, P], F32, name="b_sb%d%d" % (jt, h), align_bytes=64)
+                d_sb = sb.tile([P, half, P], F32, name="d_sb%d%d" % (jt, h), align_bytes=64)
+                nc.scalar.copy(b_sb[:], b_ps[jt][:].rearrange("j (m t) -> j t m", t=PACK)[:, ts, :])
+                nc.vector.tensor_tensor(
+                    d_sb[:], a_ps[jt][:].rearrange("j (m t) -> j t m", t=PACK)[:, ts, :], b_sb[:], ALU.subtract
+                )
+                for t in range(half):
+                    nc.tensor.transpose(bank[:, h * half + t, :], d_sb[:, t, :], ident[:])
+            turned.append(bank)
+
+        p_ps = [psum.tile([P, J], F32, name="p_ps%d" % nt) for nt in range(NT)]
+        p_sb = [sb.tile([P, J], F32, name="p_sb%d" % nt, align_bytes=64) for nt in range(NT)]
+        for jt in range(JT):
+            hid = sb.tile([P, P, PACK], BF16, name="hid%d" % jt, align_bytes=64)
+            nc.scalar.activation(hid[:], turned[jt][:].rearrange("p t j -> p j t"), ACT.Abs)
+            hid_w = sb.tile([P, P], U32, name="hid_w%d" % jt, align_bytes=64)
+            hid_s = sb.tile([P, P], U8, name="hid_s%d" % jt, align_bytes=64)
+            nc.vector.quantize_mx(
+                out=hid_w[:].bitcast(E5M2), scales=hid_s[:], in_=hid[:].rearrange("p j t -> p (j t)")
+            )
+            js = slice(jt * P, (jt + 1) * P)
+            for nt in range(NT):
+                ns = slice(nt * P, (nt + 1) * P)
+                nc.tensor.matmul_mx(
+                    out=p_ps[nt][:, js], lhsT=wb_w[:, ns].bitcast(E2M1), lhsT_scale=wb_s[:, ns],
+                    rhs=hid_w[:].bitcast(E5M2), rhs_scale=hid_s[:], start=True, stop=True,
+                )
+            nc.scalar.copy(p_sb[0][:, js], p_ps[0][:, js])
+            nc.vector.tensor_copy(p_sb[1][:, js], p_ps[1][:, js])
+
+        picked = [[sb.tile([P, E], F32, name="pick%d%d" % (nt, u), align_bytes=64) for u in range(2)] for nt in range(NT)]
+        for u, index in enumerate((idx3, idx4)):
+            nc.scalar.activation(picked[0][u][:], p_sb[0][:].indirect(index[:]), ACT.Copy)
+            nc.vector.tensor_copy(picked[1][u][:], p_sb[1][:].indirect(index[:]))
+        for nt, queue in ((1, nc.sync), (0, nc.scalar)):
+            best = sb.tile([P, E], F32, name="best%d" % nt, align_bytes=64)
+            nc.vector.tensor_tensor(best[:], picked[nt][0][:], picked[nt][1][:], ALU.max)
+            queue.dma_start(out[nt * P : (nt + 1) * P, :], best[:])

@@ -85,7 +85,7 @@ def tile_list_crossed_direct_one_bestoftwo_kernel(
         w2_w = load_fp8_words(w2_words, "w2_w")
         idx = load_list(offs, "idx")
         xt_w = load_fp4_words(xt_words, "xt_w")
-        load_scales(xt_s, xt_scales, [nc.gpsimd] * 3 + [nc.sync])
+        load_scales(xt_s, xt_scales, [nc.sync] * 4)
         load_scales(wb_s, wb_scales, [nc.sync] * 4)
         wb_w = load_fp4_words(wb_words, "wb_w")
         idx3 = load_list(offs3, "idx3")
@@ -161,7 +161,7 @@ def tile_list_crossed_direct_one_bestoftwo_kernel(
         for u, index in enumerate((idx3, idx4)):
             nc.scalar.activation(picked[0][u][:], p_sb[0][:].indirect(index[:]), ACT.Copy)
             nc.vector.tensor_copy(picked[1][u][:], p_sb[1][:].indirect(index[:]))
-        for nt, queue in ((1, nc.sync), (0, nc.scalar)):
+        for nt, queue in ((0, nc.scalar), (1, nc.sync)):
             best = sb.tile([P, E], F32, name="best%d" % nt, align_bytes=64)
             nc.vector.tensor_tensor(best[:], picked[nt][0][:], picked[nt][1][:], ALU.max)
             queue.dma_start(out[nt * P : (nt + 1) * P, :], best[:])

@@ -46,9 +46,9 @@ def tile_list_crossed_direct_one_bestoftwo_kernel(
             nc.vector.memset(plane[:].bitcast(I32), 0)
             return plane
 
-        def load_scales(plane, src, queues):
-            for q, queue in enumerate(queues):
-                queue.dma_start(
+        def load_scales(plane, src, quadrants):
+            for q in quadrants:
+                nc.sync.dma_start(
                     plane[QUADRANT * q : QUADRANT * q + PACK, :].bitcast(I32),
                     src[0, PACK * q : PACK * (q + 1), :].bitcast(I32),
                 )
@@ -74,19 +74,19 @@ def tile_list_crossed_direct_one_bestoftwo_kernel(
         nc.sync.dma_start(both_s[0:rows, 0:R].bitcast(I32), w2_scales[0].bitcast(I32))
         nc.sync.dma_start(both_s[0:rows, R : 2 * R].bitcast(I32), w_scales[0].bitcast(I32))
         idx2 = load_list(offs2, "idx2")
-        load_scales(xo_s, xo_scales, [nc.sync] * 4)
+        load_scales(xo_s, xo_scales, range(4))
         xo_w = load_fp8_words(xo_words, "xo_w")
-        w_w = load_fp8_words(w_words, "w_w")
+        idx = load_list(offs, "idx")
         for q in range(1, P // QUADRANT):
             nc.sync.dma_start(
                 both_s[QUADRANT * q : QUADRANT * q + PACK, :].bitcast(I32),
                 both_s[PACK * q : PACK * (q + 1), :].bitcast(I32),
             )
-        w2_w = load_fp8_words(w2_words, "w2_w")
-        idx = load_list(offs, "idx")
+        w_w = load_fp8_words(w_words, "w_w")
         xt_w = load_fp4_words(xt_words, "xt_w")
-        load_scales(xt_s, xt_scales, [nc.sync] * 4)
-        load_scales(wb_s, wb_scales, [nc.sync] * 4)
+        w2_w = load_fp8_words(w2_words, "w2_w")
+        load_scales(xt_s, xt_scales, range(4))
+        load_scales(wb_s, wb_scales, range(4))
         wb_w = load_fp4_words(wb_words, "wb_w")
         idx3 = load_list(offs3, "idx3")
         idx4 = load_list(offs4, "idx4")
@@ -107,7 +107,7 @@ def tile_list_crossed_direct_one_bestoftwo_kernel(
         xt_g = [gather_columns(xt_w, xt_s, idx, jt, "xt") for jt in range(JT)]
 
         a_ps = [psum.tile([P, R], F32, name="a%d" % jt) for jt in range(JT)]
-        b_ps = [psum.tile([P, R], F32, name="b%d" % jt) for jt in range(JT)]
+        b_ps = [psum.tile([P, R], F32, name="b%d" % jt, tag="b%d" % jt) for jt in range(JT)]
 
         def first_stage(acc, picked, picked_fmt, words, fmt, plane, first):
             nc.tensor.matmul_mx(
@@ -115,11 +115,14 @@ def tile_list_crossed_direct_one_bestoftwo_kernel(
                 rhs=words[:].bitcast(fmt), rhs_scale=plane, start=first, stop=not first,
             )
 
-        for jt in range(JT):
-            first_stage(b_ps[jt], xo_g[jt], E4M3, w_w, E4M3, w_s, True)
-            first_stage(a_ps[jt], xo_g[jt], E4M3, w2_w, E5M2, w2_s, True)
-            first_stage(b_ps[jt], xt_g[jt], E2M1, w2_w, E5M2, w2_s, False)
-            first_stage(a_ps[jt], xt_g[jt], E2M1, w_w, E4M3, w_s, False)
+        first_stage(b_ps[0], xo_g[0], E4M3, w_w, E4M3, w_s, True)
+        first_stage(a_ps[0], xo_g[0], E4M3, w2_w, E5M2, w2_s, True)
+        first_stage(b_ps[0], xt_g[0], E2M1, w2_w, E5M2, w2_s, False)
+        first_stage(a_ps[0], xt_g[0], E2M1, w_w, E4M3, w_s, False)
+        first_stage(b_ps[1], xo_g[1], E4M3, w_w, E4M3, w_s, True)
+        first_stage(b_ps[1], xt_g[1], E2M1, w2_w, E5M2, w2_s, False)
+        first_stage(a_ps[1], xt_g[1], E2M1, w_w, E4M3, w_s, True)
+        first_stage(a_ps[1], xo_g[1], E4M3, w2_w, E5M2, w2_s, False)
 
         half = PACK // 2
         turned = []
@@ -137,7 +140,10 @@ def tile_list_crossed_direct_one_bestoftwo_kernel(
                     nc.tensor.transpose(bank[:, h * half + t, :], d_sb[:, t, :], ident[:])
             turned.append(bank)
 
-        p_ps = [psum.tile([P, J], F32, name="p_ps%d" % nt) for nt in range(NT)]
+        p_first = psum.tile([P, NT, P], F32, name="p_first")
+        p_last0 = psum.tile([P, P], F32, name="p_last0")
+        p_last1 = psum.tile([P, P], F32, name="p_last1", tag="b0")
+        p_ps = [[p_first[:, 0, :], p_first[:, 1, :]], [p_last0[:], p_last1[:]]]
         p_sb = [sb.tile([P, J], F32, name="p_sb%d" % nt, align_bytes=64) for nt in range(NT)]
         for jt in range(JT):
             hid = sb.tile([P, P, PACK], BF16, name="hid%d" % jt, align_bytes=64)
@@ -148,20 +154,23 @@ def tile_list_crossed_direct_one_bestoftwo_kernel(
                 out=hid_w[:].bitcast(E5M2), scales=hid_s[:], in_=hid[:].rearrange("p j t -> p (j t)")
             )
             js = slice(jt * P, (jt + 1) * P)
-            for nt in range(NT):
+            for nt in reversed(range(NT)):
                 ns = slice(nt * P, (nt + 1) * P)
                 nc.tensor.matmul_mx(
-                    out=p_ps[nt][:, js], lhsT=wb_w[:, ns].bitcast(E2M1), lhsT_scale=wb_s[:, ns],
+                    out=p_ps[jt][nt], lhsT=wb_w[:, ns].bitcast(E2M1), lhsT_scale=wb_s[:, ns],
                     rhs=hid_w[:].bitcast(E5M2), rhs_scale=hid_s[:], start=True, stop=True,
                 )
-            nc.scalar.copy(p_sb[0][:, js], p_ps[0][:, js])
-            nc.vector.tensor_copy(p_sb[1][:, js], p_ps[1][:, js])
+            nc.scalar.copy(p_sb[0][:, js], p_ps[jt][0])
+            if jt == 0:
+                nc.scalar.copy(p_sb[1][:, js], p_ps[jt][1])
+            else:
+                nc.vector.tensor_copy(p_sb[1][:, js], p_ps[jt][1])
 
         picked = [[sb.tile([P, E], F32, name="pick%d%d" % (nt, u), align_bytes=64) for u in range(2)] for nt in range(NT)]
         for u, index in enumerate((idx3, idx4)):
             nc.scalar.activation(picked[0][u][:], p_sb[0][:].indirect(index[:]), ACT.Copy)
             nc.vector.tensor_copy(picked[1][u][:], p_sb[1][:].indirect(index[:]))
-        for nt, queue in ((0, nc.scalar), (1, nc.sync)):
+        for nt, queue in ((1, nc.sync), (0, nc.scalar)):
             best = sb.tile([P, E], F32, name="best%d" % nt, align_bytes=64)
             nc.vector.tensor_tensor(best[:], picked[nt][0][:], picked[nt][1][:], ALU.max)
             queue.dma_start(out[nt * P : (nt + 1) * P, :], best[:])

from contextlib import ExitStack

import concourse.mybir as mybir
from concourse.masks import make_identity

K, T, Z, J, R, N, E = 512, 1024, 1024, 256, 512, 256, 128
FLOPS = 4 * 2 * K * R * J + 2 * R * N * J

F32 = mybir.dt.float32
BF16 = mybir.dt.bfloat16
I32 = mybir.dt.int32
U32 = mybir.dt.uint32
U16 = mybir.dt.uint16
U8 = mybir.dt.uint8
E4M3 = mybir.dt.float8_e4m3fn_x4
E5M2 = mybir.dt.float8_e5m2_x4
E2M1 = mybir.dt.float4_e2m1fn_x4
ACT = mybir.ActivationFunctionType
ALU = mybir.AluOpType

P = 128
PACK = 4
QUADRANT = 32
LIST_ROWS = 16
JT = J // P
NT = N // P


def tile_list_crossed_direct_one_bestoftwo_kernel(
    tc, xt_words, xt_scales, xo_words, xo_scales, w_words, w_scales, w2_words, w2_scales,
    wb_words, wb_scales, offs, offs2, offs3, offs4, out
):
    nc = tc.nc
    with ExitStack() as ctx:
        lists = ctx.enter_context(tc.tile_pool(name="lists", bufs=1))
        sb = ctx.enter_context(tc.tile_pool(name="sb", bufs=1))
        psum = ctx.enter_context(tc.psum_pool(name="psum", bufs=1))

        def load_list(src, name):
            tile = lists.tile(list(src.shape), U16, name=name)
            nc.sync.dma_start(tile[:], src)
            return tile

        def zeroed_plane(width, name):
            plane = sb.tile([P, width], U8, name=name, align_bytes=64)
            nc.vector.memset(plane[:].bitcast(I32), 0)
            return plane

        def load_scales(plane, src, quadrants):
            for q in quadrants:
                nc.sync.dma_start(
                    plane[QUADRANT * q : QUADRANT * q + PACK, :].bitcast(I32),
                    src[0, PACK * q : PACK * (q + 1), :].bitcast(I32),
                )

        def load_fp8_words(src, name):
            tile = sb.tile([P, src.shape[2]], U32, name=name, align_bytes=64)
            nc.sync.dma_start(tile[:].bitcast(I32), src[0].rearrange("p n t -> p (n t)").bitcast(I32))
            return tile

        def load_fp4_words(src, name):
            tile = sb.tile([P, src.shape[2] // 2], U16, name=name, align_bytes=64)
            nc.sync.dma_start(tile[:].bitcast(I32), src[0].bitcast(I32))
            return tile

        xo_s = zeroed_plane(Z, "xo_s")
        xt_s = zeroed_plane(T, "xt_s")
        both_s = sb.tile([P, 2 * R], U8, name="both_s", align_bytes=64)
        w2_s = both_s[:, 0:R]
        w_s = both_s[:, R : 2 * R]
        wb_s = sb.tile([P, N], U8, name="wb_s", align_bytes=64)

        rows = K // 32
        nc.sync.dma_start(both_s[0:rows, 0:R].bitcast(I32), w2_scales[0].bitcast(I32))
        nc.sync.dma_start(both_s[0:rows, R : 2 * R].bitcast(I32), w_scales[0].bitcast(I32))
        idx2 = load_list(offs2, "idx2")
        load_scales(xo_s, xo_scales, range(4))
        xo_w = load_fp8_words(xo_words, "xo_w")
        idx = load_list(offs, "idx")
        for q in range(1, P // QUADRANT):
            nc.sync.dma_start(
                both_s[QUADRANT * q : QUADRANT * q + PACK, :].bitcast(I32),
                both_s[PACK * q : PACK * (q + 1), :].bitcast(I32),
            )
        w_w = load_fp8_words(w_words, "w_w")
        xt_w = load_fp4_words(xt_words, "xt_w")
        w2_w = load_fp8_words(w2_words, "w2_w")
        load_scales(xt_s, xt_scales, range(4))
        load_scales(wb_s, wb_scales, range(4))
        wb_w = load_fp4_words(wb_words, "wb_w")
        idx3 = load_list(offs3, "idx3")
        idx4 = load_list(offs4, "idx4")

        ident = sb.tile([P, P], F32, name="ident", align_bytes=64)
        make_identity(nc, ident[:])

        def gather_columns(words, plane, index, jt, name):
            cols = P // LIST_ROWS
            part = index[:, jt * cols : (jt + 1) * cols]
            g_s = sb.tile([P, P], U8, name=name + "_gs%d" % jt, align_bytes=64)
            g_w = sb.tile([P, P], words.dtype, name=name + "_gw%d" % jt, align_bytes=64)
            nc.vector.tensor_copy(g_s[:], plane[:].indirect(part))
            nc.vector.tensor_copy(g_w[:], words[:].indirect(part))
            return g_w, g_s

        xo_g = [gather_columns(xo_w, xo_s, idx2, jt, "xo") for jt in range(JT)]
        xt_g = [gather_columns(xt_w, xt_s, idx, jt, "xt") for jt in range(JT)]

        a_ps = [psum.tile([P, R], F32, name="a%d" % jt) for jt in range(JT)]
        b_ps = [psum.tile([P, R], F32, name="b%d" % jt, tag="b%d" % jt) for jt in range(JT)]

        def first_stage(acc, picked, picked_fmt, words, fmt, plane, first):
            nc.tensor.matmul_mx(
                out=acc[:], lhsT=picked[0][:].bitcast(picked_fmt), lhsT_scale=picked[1][:],
                rhs=words[:].bitcast(fmt), rhs_scale=plane, start=first, stop=not first,
            )

        first_stage(b_ps[0], xo_g[0], E4M3, w_w, E4M3, w_s, True)
        first_stage(a_ps[0], xo_g[0], E4M3, w2_w, E5M2, w2_s, True)
        first_stage(b_ps[0], xt_g[0], E2M1, w2_w, E5M2, w2_s, False)
        first_stage(a_ps[0], xt_g[0], E2M1, w_w, E4M3, w_s, False)
        first_stage(b_ps[1], xo_g[1], E4M3, w_w, E4M3, w_s, True)
        first_stage(b_ps[1], xt_g[1], E2M1, w2_w, E5M2, w2_s, False)
        first_stage(a_ps[1], xt_g[1], E2M1, w_w, E4M3, w_s, True)
        first_stage(a_ps[1], xo_g[1], E4M3, w2_w, E5M2, w2_s, False)

        half = PACK // 2
        turned = []
        for jt in range(JT):
            bank = psum.tile([P, PACK, P], F32, name="turned%d" % jt)
            for h in range(2):
                ts = slice(h * half, (h + 1) * half)
                b_sb = sb.tile([P, half, P], F32, name="b_sb%d%d" % (jt, h), align_bytes=64)
                d_sb = sb.tile([P, half, P], F32, name="d_sb%d%d" % (jt, h), align_bytes=64)
                nc.scalar.copy(b_sb[:], b_ps[jt][:].rearrange("j (m t) -> j t m", t=PACK)[:, ts, :])
                nc.vector.tensor_tensor(
                    d_sb[:], a_ps[jt][:].rearrange("j (m t) -> j t m", t=PACK)[:, ts, :], b_sb[:], ALU.subtract
                )
                for t in range(half):
                    nc.tensor.transpose(bank[:, h * half + t, :], d_sb[:, t, :], ident[:])
            turned.append(bank)

        p_first = psum.tile([P, NT, P], F32, name="p_first")
        p_last0 = psum.tile([P, P], F32, name="p_last0")
        p_last1 = psum.tile([P, P], F32, name="p_last1", tag="b0")
        p_ps = [[p_first[:, 0, :], p_first[:, 1, :]], [p_last0[:], p_last1[:]]]
        p_sb = [sb.tile([P, J], F32, name="p_sb%d" % nt, align_bytes=64) for nt in range(NT)]
        for jt in range(JT):
            hid = sb.tile([P, P, PACK], BF16, name="hid%d" % jt, align_bytes=64)
            nc.scalar.activation(hid[:], turned[jt][:].rearrange("p t j -> p j t"), ACT.Abs)
            hid_w = sb.tile([P, P], U32, name="hid_w%d" % jt, align_bytes=64)
            hid_s = sb.tile([P, P], U8, name="hid_s%d" % jt, align_bytes=64)
            nc.vector.quantize_mx(
                out=hid_w[:].bitcast(E5M2), scales=hid_s[:], in_=hid[:].rearrange("p j t -> p (j t)")
            )
            js = slice(jt * P, (jt + 1) * P)
            for nt in reversed(range(NT)):
                ns = slice(nt * P, (nt + 1) * P)
                nc.tensor.matmul_mx(
                    out=p_ps[jt][nt], lhsT=wb_w[:, ns].bitcast(E2M1), lhsT_scale=wb_s[:, ns],
                    rhs=hid_w[:].bitcast(E5M2), rhs_scale=hid_s[:], start=True, stop=True,
                )
            nc.scalar.copy(p_sb[0][:, js], p_ps[jt][0])
            if jt == 0:
                nc.scalar.copy(p_sb[1][:, js], p_ps[jt][1])
            else:
                nc.vector.tensor_copy(p_sb[1][:, js], p_ps[jt][1])

        picked = [[sb.tile([P, E], F32, name="pick%d%d" % (nt, u), align_bytes=64) for u in range(2)] for nt in range(NT)]
        for u, index in enumerate((idx3, idx4)):
            nc.scalar.activation(picked[0][u][:], p_sb[0][:].indirect(index[:]), ACT.Copy)
            nc.vector.tensor_copy(picked[1][u][:], p_sb[1][:].indirect(index[:]))
        for nt, queue in ((1, nc.sync), (0, nc.scalar)):
            best = sb.tile([P, E], F32, name="best%d" % nt, align_bytes=64)
            nc.vector.tensor_tensor(best[:], picked[nt][0][:], picked[nt][1][:], ALU.max)
            queue.dma_start(out[nt * P : (nt + 1) * P, :], best[:])
